import numpy as np
import ml_dtypes


def mxq(x, axis, fmt="e4m3"):
    dtype, down = {"e4m3": (ml_dtypes.float8_e4m3fn, 7), "e5m2": (ml_dtypes.float8_e5m2, 14)}[fmt]
    v = np.moveaxis(np.asarray(x, np.float32).astype(ml_dtypes.bfloat16).astype(np.float64), axis, -1)
    blocks = v.reshape(v.shape[:-1] + (-1, 32))
    amax = np.abs(blocks).max(-1, keepdims=True)
    byte = np.maximum(np.where(amax > 0, np.frexp(amax)[1] - 1 + 127, 0) - down, 1)
    scale = np.exp2(byte - 127.0)
    codes = (blocks / scale).astype(np.float32).astype(dtype).astype(np.float64)
    return np.moveaxis((codes * scale).reshape(v.shape), -1, axis)


WIDE = False


def mx_kscale(k):
    if not WIDE:
        return np.ones(k)
    levels = np.array([10, -10, 5, -5, 0])
    if k % 512:
        return np.exp2(np.random.permutation(np.resize(levels, k // 32))).repeat(32)
    a = np.empty((k // 512, 16))
    for p in range(k // 512):
        a[p, :8] = np.random.permutation(np.resize(levels, 8))
        for g in range(8):
            far = levels[np.abs(levels - a[p, g]) >= 10]
            a[p, g + 8] = far[np.random.randint(len(far))]
    return np.exp2(a.ravel()).repeat(32)


def f64(x):
    return np.asarray(x).astype(np.float64)


def striped(idx):
    return np.tile(idx.reshape(-1, 16).T, (8, 1)).astype(np.uint16)


def unstriped(offs):
    return offs[:16].T.reshape(-1).astype(np.int64)


def pack_weight(w):
    k, n = w.shape
    w = f64(np.asarray(w, np.float32).astype(ml_dtypes.bfloat16)).reshape(k // 32, 32, n)
    amax = np.abs(w).max(1)
    byte = np.clip(np.where(amax > 0, np.frexp(amax)[1] - 1 + 127 - 7, 1), 1, 254)
    scaled = (w * np.exp2(127.0 - byte)[:, None, :]).reshape(k, n).astype(np.float32)
    words = np.ascontiguousarray(scaled.reshape(k // 512, 128, 4, n).transpose(0, 1, 3, 2)).astype(ml_dtypes.float8_e4m3fn).view(np.uint8)
    return words, np.ascontiguousarray(byte.astype(np.uint8).reshape(k // 512, 16, n))


def unpack_weight(words, scales):
    g, p, n, _ = words.shape
    vals = np.ascontiguousarray(words).view(ml_dtypes.float8_e4m3fn).astype(np.float64) * np.repeat(np.exp2(scales.astype(np.float64) - 127.0), 8, axis=1)[..., None]
    return vals.transpose(0, 1, 3, 2).reshape(g * 512, n)


def gelu(v):
    return 0.5 * v * (1.0 + np.tanh(np.sqrt(2.0 / np.pi) * (v + 0.044715 * v**3)))


K, T, S, H, Z, W = 512, 1024, 512, 512, 512, 1024
P = 2 ** 7


def setup_inputs():
    n = np.random.standard_normal
    s = mx_kscale(K)[:, None]
    u = mx_kscale(H)
    packed_xT = pack_weight(n((K, T)) * s)
    packed_eT = pack_weight(n((K, W)) * s)
    return {
        "x_words": packed_xT[0],
        "x_scales": packed_xT[1],
        "w1": (n((K, H)) / np.sqrt(K) / s).astype(np.float32),
        "w2": (n((K, H)) / np.sqrt(K) / s).astype(np.float32),
        "e_words": packed_eT[0],
        "e_scales": packed_eT[1],
        "w3": (n((K, H)) / np.sqrt(K) / s).astype(np.float32),
        "unit": (np.random.uniform(0.6, 1.4, (H, 1)) * u[:, None]).astype(np.float32),
        "unit2": (np.random.uniform(0.6, 1.4, (H, 1)) / np.sqrt(H) / u[:, None]).astype(np.float32),
        "rad": (np.tile(np.random.uniform(0.2, 1.0, W), (P, 1))).astype(np.float32),
        "offs": striped(np.random.permutation(T)[:S]),
        "obs_": striped(np.random.permutation(W)[:Z]),
        "par": striped(np.random.permutation(S)),
        "nxo": striped(np.random.permutation(Z)),
    }


def reference(x_words, x_scales, w1, w2, e_words, e_scales, w3, unit, unit2, rad, offs, obs_, par, nxo):
    xq = unpack_weight(x_words, x_scales)[:, unstriped(offs)]
    y = mxq(f64(w1), 0, "e4m3").T @ xq
    yv = mxq(f64(w2), 0, "e4m3").T @ xq
    vp = yv[:, unstriped(par)]
    pos = y + 0.6 * vp
    hid = f64(unit) * pos
    e_obs_ = unpack_weight(e_words, e_scales)[:, unstriped(obs_)]
    ye = mxq(f64(w3), 0, "e4m3").T @ e_obs_
    obst = gelu(ye)
    hid2 = f64(unit2) * obst
    sc = mxq(hid, 0, "e4m3").T @ mxq(hid2, 0, "e4m3")
    clr = np.abs(sc) + 0.1 - (f64(rad)[:1][:, unstriped(obs_)])
    pen = np.log(np.exp(-2.0 * clr) + 1.0)
    return pen + 0.5 * pen[:, unstriped(nxo)]

@@ -1,0 +1,291 @@
+from contextlib import ExitStack
+
+import concourse.mybir as mybir
+from concourse.masks import make_identity
+
+F32 = mybir.dt.float32
+BF16 = mybir.dt.bfloat16
+I32 = mybir.dt.int32
+U32 = mybir.dt.uint32
+U16 = mybir.dt.uint16
+U8 = mybir.dt.uint8
+FP8X4 = mybir.dt.float8_e4m3fn_x4
+ACT = mybir.ActivationFunctionType
+ALU = mybir.AluOpType
+
+P = 128
+PACK = 4
+N = 512
+TABLE = 1024
+HALF = N // 2
+LIST_HALF = HALF // 16
+
+FLOPS = 4 * 2 * N * N * N
+
+
+def tile_picked_ycollid_pen_p_kernel(
+    tc, x_words, x_scales, w1, w2, e_words, e_scales, w3, unit, unit2, rad, offs, obs_, par, nxo, out
+):
+    nc = tc.nc
+    with ExitStack() as ctx:
+        keep = ctx.enter_context(tc.tile_pool(name="keep", bufs=1))
+        e_room = ctx.enter_context(tc.tile_pool(name="e_room", bufs=1))
+        w3_room = ctx.enter_context(tc.tile_pool(name="w3_room", bufs=1))
+        psum = ctx.enter_context(tc.psum_pool(name="psum", bufs=1))
+
+        def sb(name, shape, dtype, tag=None):
+            return keep.tile(shape, dtype, name=name, tag=tag or name, align_bytes=64)
+
+        def placed(room, offset, name, shape, dtype):
+            return room.tile(shape, dtype, name=name, align_bytes=64, offset=offset)
+
+        def bank(b):
+            return psum.tile([P, N], F32, name=f"bank{b}")
+
+        def load_list(name, src):
+            t = sb(name, [P, N // 16], U16)
+            nc.sync.dma_start(t[:], src)
+            return t
+
+        def load_words(t, words):
+            nc.sync.dma_start(t[:], words[0].rearrange("p c r -> p (c r)").bitcast(I32))
+
+        def load_scales(t, scales, clear, queue):
+            clear.memset(t[:].bitcast(I32), 0)
+            for q in range(4):
+                queue.dma_start(
+                    t[32 * q : 32 * q + 4, :].bitcast(I32), scales[0, 4 * q : 4 * q + 4, :].bitcast(I32)
+                )
+
+        def load_weight(t, w):
+            nc.sync.dma_start(t[:], w.rearrange("(p j) c -> p j c", j=PACK))
+
+        def load_unit(name, u):
+            t = sb(name, [P, PACK], F32)
+            nc.gpsimd.dma_start(t[:], u.rearrange("(p t) o -> p (t o)", t=PACK))
+            return t
+
+        def pick(gw, gs, words, scales, lst):
+            nc.vector.tensor_copy(gw[:], words[:].bitcast(U32).indirect(lst[:]))
+            nc.vector.tensor_copy(gs[:], scales[:].indirect(lst[:]))
+            return gw, gs
+
+        def dealt(g):
+            return g[:].rearrange("p (t m j) -> p m j t", t=PACK, j=PACK)
+
+        def as_loaded(raw):
+            return raw[:].rearrange("p j (m t) -> p m j t", t=PACK)
+
+        def round_weight(copy, g, first, last, raw, raw_first=0):
+            copy(dealt(g)[:, first:last], as_loaded(raw)[:, first - raw_first : last - raw_first])
+
+        def quantize(codes, scales, src):
+            nc.vector.quantize_mx(out=codes.bitcast(FP8X4), scales=scales, in_=src)
+
+        def quantize_whole(name, g):
+            c = sb(name + "_c", [P, N], U32)
+            s = sb(name + "_s", [P, N], U8)
+            quantize(c[:], s[:], g[:])
+            return c, s
+
+        def mm(dst, lhs, lcols, rhs, rcols):
+            nc.tensor.matmul_mx(
+                out=dst,
+                lhsT=lhs[0][:, lcols].bitcast(FP8X4),
+                lhsT_scale=lhs[1][:, lcols],
+                rhs=rhs[0][:, rcols].bitcast(FP8X4),
+                rhs_scale=rhs[1][:, rcols],
+                start=True,
+                stop=True,
+            )
+
+        def block(i, width=P):
+            return slice(i * width, (i + 1) * width)
+
+        obs_l = load_list("obs_l", obs_)
+        rad_cols = sb("rad_cols", [P, TABLE // P], F32, "rad_then_x")
+        nc.scalar.dma_start(rad_cols[:], rad[0, :].rearrange("(p m) -> p m", p=P))
+        offs_l = load_list("offs_l", offs)
+        e_w = placed(e_room, 0, "e_w", [P, TABLE], I32)
+        load_words(e_w, e_words)
+        e_s = sb("e_s", [P, TABLE], U8, "e_s_then_w1")
+        load_scales(e_s, e_scales, nc.vector, nc.scalar)
+        w3_raw = sb("w3_raw", [P, PACK, N], F32, "w3_then_w1")
+        load_weight(w3_raw, w3)
+        par_l = load_list("par_l", par)
+        nxo_l = load_list("nxo_l", nxo)
+        ident = sb("ident", [P, P], F32, "ident_then_x_s")
+        make_identity(nc, ident[:])
+        unit2_t = load_unit("unit2_t", unit2)
+        unit_t = load_unit("unit_t", unit)
+
+        rad_t = sb("rad_t", [P, TABLE], F32)
+        for b in range(2):
+            spread = bank(b)
+            for m in range(4):
+                col = rad_cols[:, 4 * b + m : 4 * b + m + 1]
+                nc.tensor.transpose(spread[:, block(m)], col.to_broadcast([P, P]), ident[:])
+            nc.scalar.activation(
+                rad_t[:].rearrange("p (n m) -> p n m", m=8)[:, :, 4 * b : 4 * b + 4],
+                spread[:].rearrange("p (m n) -> p n m", m=4),
+                ACT.Copy,
+            )
+        x_w = sb("x_w", [P, TABLE], I32, "rad_then_x")
+        load_words(x_w, x_words)
+        x_s = sb("x_s", [P, TABLE], U8, "ident_then_x_s")
+        load_scales(x_s, x_scales, nc.gpsimd, nc.sync)
+        unit_par = sb("unit_par", [P, PACK], F32)
+        nc.gpsimd.tensor_scalar(unit_par[:], unit_t[:], 0.6, 0.0, ALU.mult, ALU.add)
+
+        reach = sb("reach", [P, N], F32)
+
+        def fetch_radius(name, first, last, tag=None):
+            g = sb(name, [P, last - first], F32, tag)
+            nc.scalar.activation(g[:], rad_t[:].indirect(obs_l[:, first // 16 : last // 16]), ACT.Copy)
+            return g
+
+        def make_reach(g, first, last):
+            nc.scalar.activation(reach[:, first:last], g[:], ACT.Exp, scale=2.0, bias=-0.2)
+
+        rad_a = fetch_radius("rad_a", 0, 224)
+        rad_b = fetch_radius("rad_b", 224, 448)
+        make_reach(rad_a, 0, 224)
+        make_reach(rad_b, 224, 448)
+
+        eq_w = sb("eq_w", [P, N], U32, "eq_then_w1")
+        eq_s = placed(e_room, 0, "eq_s", [P, N], U8)
+        eq = pick(eq_w, eq_s, e_w, e_s, obs_l)
+        w2_raw = placed(e_room, 512, "w2_raw", [P, PACK, N], F32)
+        load_weight(w2_raw, w2)
+        w1_lo = sb("w1_lo", [P, PACK, HALF], F32, "e_s_then_w1")
+        load_weight(w1_lo, w1[:, 0:HALF])
+        w3_bf = placed(w3_room, 0, "w3_bf", [P, PACK * N], BF16)
+        round_weight(nc.scalar.copy, w3_bf, 0, 44, w3_raw)
+        round_weight(nc.vector.tensor_copy, w3_bf, 44, P, w3_raw)
+        w1_hi = sb("w1_hi", [P, PACK, HALF], F32, "w3_then_w1")
+        load_weight(w1_hi, w1[:, HALF:N])
+        w3q = quantize_whole("w3q", w3_bf)
+        obst = []
+        for t in range(PACK):
+            ye = bank(4 + t)
+            mm(ye[:], w3q, block(t), eq, slice(0, N))
+            o = sb(f"obst{t}", [P, N], F32)
+            nc.scalar.activation(o[:], ye[:], ACT.Gelu_apprx_tanh)
+            obst.append(o)
+
+        xq_w = placed(w3_room, 0, "xq_w", [P, N], U32)
+        xq_s = placed(w3_room, 2048, "xq_s", [P, N], U8)
+        xq = pick(xq_w, xq_s, x_w, x_s, offs_l)
+        w2_bf = sb("w2_bf", [P, PACK * N], BF16, "ident_then_x_s")
+        round_weight(nc.vector.tensor_copy, w2_bf, 0, P, w2_raw)
+        hid2_planes = placed(e_room, 512, "hid2_planes", [P, PACK, N], F32)
+
+        def scale_obst(t):
+            nc.vector.tensor_scalar(hid2_planes[:, t, :], obst[t][:], unit2_t[:, t : t + 1], None, ALU.mult)
+
+        def weave(name, planes):
+            g = sb(name, [P, PACK * planes.shape[2]], BF16)
+            nc.vector.tensor_copy(
+                g[:].rearrange("p (c i t) -> p c t i", i=4, t=PACK),
+                planes[:].rearrange("p t (c i) -> p c t i", i=4),
+            )
+            return g
+
+        scale_obst(0)
+        w2q = quantize_whole("w2q", w2_bf)
+        w1_bf = sb("w1_bf", [P, PACK * N], BF16, "eq_then_w1")
+        round_weight(nc.scalar.copy, w1_bf, 0, 64, w1_lo)
+        round_weight(nc.scalar.copy, w1_bf, 64, 96, w1_hi, 64)
+        yv = []
+        for t in range(PACK):
+            acc = bank(t)
+            mm(acc[:], w2q, block(t), xq, slice(0, N))
+            v = sb(f"yv{t}", [P, N], F32, "yv_then_rad" if t == 1 else None)
+            nc.scalar.activation(v[:], acc[:], ACT.Copy, scale=unit_par[:, t : t + 1])
+            yv.append(v)
+        for c in range(1, 4):
+            scale_obst(c)
+        hid2 = weave("hid2", hid2_planes)
+        round_weight(nc.vector.tensor_copy, w1_bf, 96, P, w1_hi, 64)
+        hid2q = quantize_whole("hid2q", hid2)
+        w1q = quantize_whole("w1q", w1_bf)
+        y = []
+        for t in range(PACK):
+            acc = bank(t)
+            mm(acc[:], w1q, block(t), xq, slice(0, N))
+            y.append(acc)
+
+        vp = [[sb(f"vp{h}_{t}", [P, HALF], F32) for t in range(PACK)] for h in range(2)]
+
+        def fetch_parent(h, t, on_scalar):
+            picked = yv[t][:].indirect(par_l[:, block(h, LIST_HALF)])
+            if on_scalar:
+                nc.scalar.activation(vp[h][t][:], picked, ACT.Copy)
+            else:
+                nc.vector.tensor_copy(vp[h][t][:], picked)
+
+        hid_c = sb("hid_c", [P, N], U32)
+        hid_s = sb("hid_s", [P, N], U8)
+
+        planes = [sb(f"hid_planes{h}", [P, PACK, HALF], F32) for h in range(2)]
+
+        def join(h, t):
+            nc.vector.scalar_tensor_tensor(
+                planes[h][:, t, :], y[t][:, block(h, HALF)], unit_t[:, t : t + 1], vp[h][t][:], ALU.mult, ALU.add
+            )
+
+        for t in range(PACK):
+            fetch_parent(0, t, True)
+        for t in range(PACK):
+            fetch_parent(1, t, t < 2)
+        make_reach(fetch_radius("rad_c", 448, N, "yv_then_rad"), 448, N)
+        for t in range(PACK):
+            join(0, t)
+        hid0 = weave("hid0", planes[0])
+        join(1, 0)
+        quantize(hid_c[:, block(0, HALF)], hid_s[:, block(0, HALF)], hid0[:])
+        for t in range(1, PACK):
+            join(1, t)
+        hid1 = weave("hid1", planes[1])
+        quantize(hid_c[:, block(1, HALF)], hid_s[:, block(1, HALF)], hid1[:])
+
+        decay = []
+        for r in range(4):
+            sc = bank(4 + r)
+            mm(sc[:], (hid_c, hid_s), block(r), hid2q, slice(0, N))
+            a = sb(f"mag{r}", [P, N], F32, "mag_then_expo" if r == 3 else None)
+            nc.scalar.activation(a[:], sc[:], ACT.Abs)
+            e = sb(f"decay{r}", [P, N], F32)
+            nc.scalar.activation(e[:], a[:], ACT.Exp, scale=-2.0)
+            decay.append(e)
+
+        pen = []
+        expo = sb("expo", [P, 4, N], F32, "mag_then_expo")
+        for r in range(4):
+            nc.vector.tensor_tensor(expo[:, r, :], decay[r][:], reach[:], ALU.mult)
+            p = sb(f"pen{r}", [P, N], F32)
+            nc.scalar.activation(p[:], expo[:, r, :], ACT.Ln, bias=1.0)
+            pen.append(p)
+
+        for r in range(4):
+            res = sb(f"res{r}", [P, N], F32)
+            if r < 2:
+                half_pen = sb(f"half_pen{r}", [P, N], F32)
+                nc.vector.tensor_scalar(half_pen[:], pen[r][:], 0.5, None, ALU.mult)
+                for h in range(2):
+                    nc.vector.tensor_tensor(
+                        res[:, block(h, HALF)],
+                        half_pen[:].indirect(nxo_l[:, block(h, LIST_HALF)]),
+                        pen[r][:, block(h, HALF)],
+                        ALU.add,
+                    )
+                nc.sync.dma_start(out[block(r), :], res[:])
+            else:
+                nxt = sb(f"next{r}", [P, N], F32)
+                for h in range(2):
+                    cols = block(h, HALF)
+                    nc.scalar.activation(nxt[:, cols], pen[r][:].indirect(nxo_l[:, block(h, LIST_HALF)]), ACT.Copy)
+                    nc.vector.scalar_tensor_tensor(
+                        res[:, cols], nxt[:, cols], 0.5, pen[r][:, cols], ALU.mult, ALU.add
+                    )
+                    nc.sync.dma_start(out[block(r), cols], res[:, cols])

@@ -29,8 +29,8 @@ def tile_picked_ycollid_pen_p_kernel(
     nc = tc.nc
     with ExitStack() as ctx:
         keep = ctx.enter_context(tc.tile_pool(name="keep", bufs=1))
-        e_room = ctx.enter_context(tc.tile_pool(name="e_room", bufs=1))
         w3_room = ctx.enter_context(tc.tile_pool(name="w3_room", bufs=1))
+        pen_room = ctx.enter_context(tc.tile_pool(name="pen_room", bufs=1))
         psum = ctx.enter_context(tc.psum_pool(name="psum", bufs=1))
 
         def sb(name, shape, dtype, tag=None):
@@ -50,12 +50,12 @@ def tile_picked_ycollid_pen_p_kernel(
         def load_words(t, words):
             nc.sync.dma_start(t[:], words[0].rearrange("p c r -> p (c r)").bitcast(I32))
 
-        def load_scales(t, scales, clear, queue):
-            clear.memset(t[:].bitcast(I32), 0)
+        def scale_rows(t, q):
+            return t[32 * q : 32 * q + 4, :].bitcast(I32)
+
+        def load_scales(t, scales):
             for q in range(4):
-                queue.dma_start(
-                    t[32 * q : 32 * q + 4, :].bitcast(I32), scales[0, 4 * q : 4 * q + 4, :].bitcast(I32)
-                )
+                nc.sync.dma_start(scale_rows(t, q), scales[0, 4 * q : 4 * q + 4, :].bitcast(I32))
 
         def load_weight(t, w):
             nc.sync.dma_start(t[:], w.rearrange("(p j) c -> p j c", j=PACK))
@@ -83,8 +83,8 @@ def tile_picked_ycollid_pen_p_kernel(
             nc.vector.quantize_mx(out=codes.bitcast(FP8X4), scales=scales, in_=src)
 
         def quantize_whole(name, g):
-            c = sb(name + "_c", [P, N], U32)
-            s = sb(name + "_s", [P, N], U8)
+            c = sb(name + "_c", [P, g.shape[1] // PACK], U32)
+            s = sb(name + "_s", [P, g.shape[1] // PACK], U8)
             quantize(c[:], s[:], g[:])
             return c, s
 
@@ -103,18 +103,35 @@ def tile_picked_ycollid_pen_p_kernel(
             return slice(i * width, (i + 1) * width)
 
         obs_l = load_list("obs_l", obs_)
-        rad_cols = sb("rad_cols", [P, TABLE // P], F32, "rad_then_x")
+        rad_cols = placed(w3_room, 0, "rad_cols", [P, TABLE // P], F32)
         nc.scalar.dma_start(rad_cols[:], rad[0, :].rearrange("(p m) -> p m", p=P))
-        offs_l = load_list("offs_l", offs)
-        e_w = placed(e_room, 0, "e_w", [P, TABLE], I32)
+        e_s_rows = sb("e_s_rows", [P, TABLE], U8)
+        load_scales(e_s_rows, e_scales)
+        w3_lo = sb("w3_lo", [P, PACK, HALF], F32)
+        load_weight(w3_lo, w3[:, 0:HALF])
+        e_w = sb("e_w", [P, TABLE], I32)
         load_words(e_w, e_words)
-        e_s = sb("e_s", [P, TABLE], U8, "e_s_then_w1")
-        load_scales(e_s, e_scales, nc.vector, nc.scalar)
-        w3_raw = sb("w3_raw", [P, PACK, N], F32, "w3_then_w1")
-        load_weight(w3_raw, w3)
+        offs_l = load_list("offs_l", offs)
+        w3_hi = sb("w3_hi", [P, PACK, HALF], F32)
+        load_weight(w3_hi, w3[:, HALF:N])
+        e_s = sb("e_s", [P, TABLE], U8)
+        nc.vector.memset(e_s[:].bitcast(I32), 0)
+        for q in range(4):
+            nc.vector.tensor_copy(scale_rows(e_s, q), scale_rows(e_s_rows, q))
+        x_w = sb("x_w", [P, TABLE], I32)
+        load_words(x_w, x_words)
+        x_s = sb("x_s", [P, TABLE], U8, "x_s_then_w2")
+        nc.vector.memset(x_s[:].bitcast(I32), 0)
+        load_scales(x_s, x_scales)
+        w2_raw = sb("w2_raw", [P, PACK, N], F32, "w2_then_hid2")
+        load_weight(w2_raw, w2)
+        w1_lo = sb("w1_lo", [P, PACK, HALF], F32)
+        load_weight(w1_lo, w1[:, 0:HALF])
+        w1_hi = sb("w1_hi", [P, PACK, HALF], F32)
+        load_weight(w1_hi, w1[:, HALF:N])
         par_l = load_list("par_l", par)
         nxo_l = load_list("nxo_l", nxo)
-        ident = sb("ident", [P, P], F32, "ident_then_x_s")
+        ident = sb("ident", [P, P], F32)
         make_identity(nc, ident[:])
         unit2_t = load_unit("unit2_t", unit2)
         unit_t = load_unit("unit_t", unit)
@@ -125,107 +142,71 @@ def tile_picked_ycollid_pen_p_kernel(
             for m in range(4):
                 col = rad_cols[:, 4 * b + m : 4 * b + m + 1]
                 nc.tensor.transpose(spread[:, block(m)], col.to_broadcast([P, P]), ident[:])
-            nc.scalar.activation(
+            nc.scalar.copy(
                 rad_t[:].rearrange("p (n m) -> p n m", m=8)[:, :, 4 * b : 4 * b + 4],
                 spread[:].rearrange("p (m n) -> p n m", m=4),
-                ACT.Copy,
             )
-        x_w = sb("x_w", [P, TABLE], I32, "rad_then_x")
-        load_words(x_w, x_words)
-        x_s = sb("x_s", [P, TABLE], U8, "ident_then_x_s")
-        load_scales(x_s, x_scales, nc.gpsimd, nc.sync)
         unit_par = sb("unit_par", [P, PACK], F32)
         nc.gpsimd.tensor_scalar(unit_par[:], unit_t[:], 0.6, 0.0, ALU.mult, ALU.add)
 
-        reach = sb("reach", [P, N], F32)
-
-        def fetch_radius(name, first, last, tag=None):
-            g = sb(name, [P, last - first], F32, tag)
-            nc.scalar.activation(g[:], rad_t[:].indirect(obs_l[:, first // 16 : last // 16]), ACT.Copy)
-            return g
-
-        def make_reach(g, first, last):
-            nc.scalar.activation(reach[:, first:last], g[:], ACT.Exp, scale=2.0, bias=-0.2)
-
-        rad_a = fetch_radius("rad_a", 0, 224)
-        rad_b = fetch_radius("rad_b", 224, 448)
-        make_reach(rad_a, 0, 224)
-        make_reach(rad_b, 224, 448)
-
-        eq_w = sb("eq_w", [P, N], U32, "eq_then_w1")
-        eq_s = placed(e_room, 0, "eq_s", [P, N], U8)
+        eq_w = sb("eq_w", [P, N], U32, "eq_w_then_w1")
+        eq_s = sb("eq_s", [P, N], U8, "eq_s_then_rad")
         eq = pick(eq_w, eq_s, e_w, e_s, obs_l)
-        w2_raw = placed(e_room, 512, "w2_raw", [P, PACK, N], F32)
-        load_weight(w2_raw, w2)
-        w1_lo = sb("w1_lo", [P, PACK, HALF], F32, "e_s_then_w1")
-        load_weight(w1_lo, w1[:, 0:HALF])
         w3_bf = placed(w3_room, 0, "w3_bf", [P, PACK * N], BF16)
-        round_weight(nc.scalar.copy, w3_bf, 0, 44, w3_raw)
-        round_weight(nc.vector.tensor_copy, w3_bf, 44, P, w3_raw)
-        w1_hi = sb("w1_hi", [P, PACK, HALF], F32, "w3_then_w1")
-        load_weight(w1_hi, w1[:, HALF:N])
+        round_weight(nc.scalar.copy, w3_bf, 0, 64, w3_lo)
+        round_weight(nc.scalar.copy, w3_bf, 64, 88, w3_hi, 64)
+        round_weight(nc.vector.tensor_copy, w3_bf, 88, P, w3_hi, 64)
         w3q = quantize_whole("w3q", w3_bf)
-        obst = []
+        obst = sb("obst", [P, PACK, N], F32)
         for t in range(PACK):
             ye = bank(4 + t)
             mm(ye[:], w3q, block(t), eq, slice(0, N))
-            o = sb(f"obst{t}", [P, N], F32)
-            nc.scalar.activation(o[:], ye[:], ACT.Gelu_apprx_tanh)
-            obst.append(o)
+            nc.scalar.activation(obst[:, t, :], ye[:], ACT.Gelu_apprx_tanh)
 
         xq_w = placed(w3_room, 0, "xq_w", [P, N], U32)
         xq_s = placed(w3_room, 2048, "xq_s", [P, N], U8)
         xq = pick(xq_w, xq_s, x_w, x_s, offs_l)
-        w2_bf = sb("w2_bf", [P, PACK * N], BF16, "ident_then_x_s")
+        w2_bf = sb("w2_bf", [P, PACK * N], BF16, "x_s_then_w2")
         round_weight(nc.vector.tensor_copy, w2_bf, 0, P, w2_raw)
-        hid2_planes = placed(e_room, 512, "hid2_planes", [P, PACK, N], F32)
+        hid2_planes = sb("hid2_planes", [P, PACK, N], F32, "w2_then_hid2")
 
         def scale_obst(t):
-            nc.vector.tensor_scalar(hid2_planes[:, t, :], obst[t][:], unit2_t[:, t : t + 1], None, ALU.mult)
+            nc.vector.tensor_scalar(hid2_planes[:, t, :], obst[:, t, :], unit2_t[:, t : t + 1], None, ALU.mult)
 
         def weave(name, planes):
             g = sb(name, [P, PACK * planes.shape[2]], BF16)
             nc.vector.tensor_copy(
                 g[:].rearrange("p (c i t) -> p c t i", i=4, t=PACK),
-                planes[:].rearrange("p t (c i) -> p c t i", i=4),
+                planes.rearrange("p t (c i) -> p c t i", i=4),
             )
             return g
 
         scale_obst(0)
         w2q = quantize_whole("w2q", w2_bf)
-        w1_bf = sb("w1_bf", [P, PACK * N], BF16, "eq_then_w1")
+        w1_bf = sb("w1_bf", [P, PACK * N], BF16, "eq_w_then_w1")
         round_weight(nc.scalar.copy, w1_bf, 0, 64, w1_lo)
-        round_weight(nc.scalar.copy, w1_bf, 64, 96, w1_hi, 64)
+        rad_g = sb("rad_g", [P, N], F32, "eq_s_then_rad")
+        nc.scalar.activation(rad_g[:], rad_t[:].indirect(obs_l[:]), ACT.Copy, scale=0.5)
         yv = []
         for t in range(PACK):
             acc = bank(t)
             mm(acc[:], w2q, block(t), xq, slice(0, N))
-            v = sb(f"yv{t}", [P, N], F32, "yv_then_rad" if t == 1 else None)
+            v = sb(f"yv{t}", [P, N], F32, "yv_then_reach" if t == 3 else None)
             nc.scalar.activation(v[:], acc[:], ACT.Copy, scale=unit_par[:, t : t + 1])
             yv.append(v)
-        for c in range(1, 4):
-            scale_obst(c)
-        hid2 = weave("hid2", hid2_planes)
-        round_weight(nc.vector.tensor_copy, w1_bf, 96, P, w1_hi, 64)
-        hid2q = quantize_whole("hid2q", hid2)
+        scale_obst(1)
+        scale_obst(2)
+        round_weight(nc.vector.tensor_copy, w1_bf, 64, P, w1_hi, 64)
+        scale_obst(3)
         w1q = quantize_whole("w1q", w1_bf)
         y = []
         for t in range(PACK):
-            acc = bank(t)
+            acc = bank(4 + t)
             mm(acc[:], w1q, block(t), xq, slice(0, N))
             y.append(acc)
+        hid2 = weave("hid2", hid2_planes[:])
 
         vp = [[sb(f"vp{h}_{t}", [P, HALF], F32) for t in range(PACK)] for h in range(2)]
-
-        def fetch_parent(h, t, on_scalar):
-            picked = yv[t][:].indirect(par_l[:, block(h, LIST_HALF)])
-            if on_scalar:
-                nc.scalar.activation(vp[h][t][:], picked, ACT.Copy)
-            else:
-                nc.vector.tensor_copy(vp[h][t][:], picked)
-
-        hid_c = sb("hid_c", [P, N], U32)
-        hid_s = sb("hid_s", [P, N], U8)
 
         planes = [sb(f"hid_planes{h}", [P, PACK, HALF], F32) for h in range(2)]
 
@@ -234,37 +215,51 @@ def tile_picked_ycollid_pen_p_kernel(
                 planes[h][:, t, :], y[t][:, block(h, HALF)], unit_t[:, t : t + 1], vp[h][t][:], ALU.mult, ALU.add
             )
 
-        for t in range(PACK):
-            fetch_parent(0, t, True)
-        for t in range(PACK):
-            fetch_parent(1, t, t < 2)
-        make_reach(fetch_radius("rad_c", 448, N, "yv_then_rad"), 448, N)
-        for t in range(PACK):
-            join(0, t)
-        hid0 = weave("hid0", planes[0])
-        join(1, 0)
-        quantize(hid_c[:, block(0, HALF)], hid_s[:, block(0, HALF)], hid0[:])
-        for t in range(1, PACK):
-            join(1, t)
-        hid1 = weave("hid1", planes[1])
-        quantize(hid_c[:, block(1, HALF)], hid_s[:, block(1, HALF)], hid1[:])
+        def quantize_half(h):
+            woven = [weave(f"hid{2 * h + u}", planes[h][:, :, block(u)]) for u in range(2)]
+            return [quantize_whole(f"hidq{2 * h + u}", woven[u]) for u in range(2)]
 
-        decay = []
-        for r in range(4):
-            sc = bank(4 + r)
-            mm(sc[:], (hid_c, hid_s), block(r), hid2q, slice(0, N))
-            a = sb(f"mag{r}", [P, N], F32, "mag_then_expo" if r == 3 else None)
-            nc.scalar.activation(a[:], sc[:], ACT.Abs)
-            e = sb(f"decay{r}", [P, N], F32)
-            nc.scalar.activation(e[:], a[:], ACT.Exp, scale=-2.0)
-            decay.append(e)
+        for h in range(2):
+            for t in range(PACK):
+                nc.scalar.activation(vp[h][t][:], yv[t][:].indirect(par_l[:, block(h, LIST_HALF)]), ACT.Copy)
+        reach = sb("reach", [P, N], F32, "yv_then_reach")
+        nc.scalar.activation(reach[:], rad_g[:], ACT.Exp, scale=4.0, bias=-0.2)
+        join(0, 0)
+        join(0, 1)
+        hid2q = quantize_whole("hid2q", hid2)
+        join(0, 2)
+        join(0, 3)
+        hidq = quantize_half(0)
+        for t in range(PACK):
+            join(1, t)
+        hidq = hidq + quantize_half(1)
+
+        expo = []
+        for r in range(2):
+            sc = bank(r)
+            mm(sc[:], hidq[r], slice(0, P), hid2q, slice(0, N))
+            mag = sb(f"mag{r}", [P, N], F32)
+            nc.scalar.activation(mag[:], sc[:], ACT.Abs)
+            decay = sb(f"decay{r}", [P, N], F32)
+            nc.scalar.activation(decay[:], mag[:], ACT.Exp, scale=-2.0)
+            e = sb(f"expo{r}", [P, N], F32)
+            nc.vector.tensor_tensor(e[:], decay[:], reach[:], ALU.mult)
+            expo.append(e)
+        half_clr = placed(pen_room, 1024, "half_clr", [P, 2, N], F32)
+        for r in range(2, 4):
+            sc = bank(r)
+            mm(sc[:], hidq[r], slice(0, P), hid2q, slice(0, N))
+            part = sb(f"part{r}", [P, N], F32)
+            nc.vector.scalar_tensor_tensor(part[:], sc[:], 0.5, rad_g[:], ALU.mult, ALU.add)
+            nc.vector.scalar_tensor_tensor(half_clr[:, r - 2, :], sc[:], 0.0, part[:], ALU.max, ALU.subtract)
+            e = sb(f"expo{r}", [P, N], F32)
+            nc.scalar.activation(e[:], half_clr[:, r - 2, :], ACT.Exp, scale=-4.0, bias=-0.2)
+            expo.append(e)
 
         pen = []
-        expo = sb("expo", [P, 4, N], F32, "mag_then_expo")
         for r in range(4):
-            nc.vector.tensor_tensor(expo[:, r, :], decay[r][:], reach[:], ALU.mult)
-            p = sb(f"pen{r}", [P, N], F32)
-            nc.scalar.activation(p[:], expo[:, r, :], ACT.Ln, bias=1.0)
+            p = placed(pen_room, r * N * 4, f"pen{r}", [P, N], F32)
+            nc.scalar.activation(p[:], expo[r][:], ACT.Ln, bias=1.0)
             pen.append(p)
 
         for r in range(4):

@@ -30,6 +30,7 @@ def tile_picked_ycollid_pen_p_kernel(
     with ExitStack() as ctx:
         keep = ctx.enter_context(tc.tile_pool(name="keep", bufs=1))
         w3_room = ctx.enter_context(tc.tile_pool(name="w3_room", bufs=1))
+        raw_room = ctx.enter_context(tc.tile_pool(name="raw_room", bufs=1))
         pen_room = ctx.enter_context(tc.tile_pool(name="pen_room", bufs=1))
         psum = ctx.enter_context(tc.psum_pool(name="psum", bufs=1))
 
@@ -65,10 +66,8 @@ def tile_picked_ycollid_pen_p_kernel(
             nc.gpsimd.dma_start(t[:], u.rearrange("(p t) o -> p (t o)", t=PACK))
             return t
 
-        def pick(gw, gs, words, scales, lst):
-            nc.vector.tensor_copy(gw[:], words[:].bitcast(U32).indirect(lst[:]))
-            nc.vector.tensor_copy(gs[:], scales[:].indirect(lst[:]))
-            return gw, gs
+        def pick(picked, table, lst):
+            nc.vector.tensor_copy(picked[:], table.indirect(lst[:]))
 
         def dealt(g):
             return g[:].rearrange("p (t m j) -> p m j t", t=PACK, j=PACK)
@@ -76,8 +75,8 @@ def tile_picked_ycollid_pen_p_kernel(
         def as_loaded(raw):
             return raw[:].rearrange("p j (m t) -> p m j t", t=PACK)
 
-        def round_weight(copy, g, first, last, raw, raw_first=0):
-            copy(dealt(g)[:, first:last], as_loaded(raw)[:, first - raw_first : last - raw_first])
+        def round_weight(copy, g, raw, first, last):
+            copy(dealt(g)[:, first:last], as_loaded(raw)[:, first:last])
 
         def quantize(codes, scales, src):
             nc.vector.quantize_mx(out=codes.bitcast(FP8X4), scales=scales, in_=src)
@@ -107,13 +106,11 @@ def tile_picked_ycollid_pen_p_kernel(
         nc.scalar.dma_start(rad_cols[:], rad[0, :].rearrange("(p m) -> p m", p=P))
         e_s_rows = sb("e_s_rows", [P, TABLE], U8)
         load_scales(e_s_rows, e_scales)
-        w3_lo = sb("w3_lo", [P, PACK, HALF], F32)
-        load_weight(w3_lo, w3[:, 0:HALF])
+        w3_raw = placed(raw_room, 0, "w3_raw", [P, PACK, N], F32)
+        load_weight(w3_raw, w3)
         e_w = sb("e_w", [P, TABLE], I32)
         load_words(e_w, e_words)
         offs_l = load_list("offs_l", offs)
-        w3_hi = sb("w3_hi", [P, PACK, HALF], F32)
-        load_weight(w3_hi, w3[:, HALF:N])
         e_s = sb("e_s", [P, TABLE], U8)
         nc.vector.memset(e_s[:].bitcast(I32), 0)
         for q in range(4):
@@ -125,10 +122,8 @@ def tile_picked_ycollid_pen_p_kernel(
         load_scales(x_s, x_scales)
         w2_raw = sb("w2_raw", [P, PACK, N], F32, "w2_then_hid2")
         load_weight(w2_raw, w2)
-        w1_lo = sb("w1_lo", [P, PACK, HALF], F32)
-        load_weight(w1_lo, w1[:, 0:HALF])
-        w1_hi = sb("w1_hi", [P, PACK, HALF], F32)
-        load_weight(w1_hi, w1[:, HALF:N])
+        w1_raw = sb("w1_raw", [P, PACK, N], F32)
+        load_weight(w1_raw, w1)
         par_l = load_list("par_l", par)
         nxo_l = load_list("nxo_l", nxo)
         ident = sb("ident", [P, P], F32)
@@ -149,13 +144,16 @@ def tile_picked_ycollid_pen_p_kernel(
         unit_par = sb("unit_par", [P, PACK], F32)
         nc.gpsimd.tensor_scalar(unit_par[:], unit_t[:], 0.6, 0.0, ALU.mult, ALU.add)
 
-        eq_w = sb("eq_w", [P, N], U32, "eq_w_then_w1")
-        eq_s = sb("eq_s", [P, N], U8, "eq_s_then_rad")
-        eq = pick(eq_w, eq_s, e_w, e_s, obs_l)
+        eq_s = sb("eq_s", [P, N], U8, "eq_s_then_reach")
+        pick(eq_s, e_s[:], obs_l)
         w3_bf = placed(w3_room, 0, "w3_bf", [P, PACK * N], BF16)
-        round_weight(nc.scalar.copy, w3_bf, 0, 64, w3_lo)
-        round_weight(nc.scalar.copy, w3_bf, 64, 88, w3_hi, 64)
-        round_weight(nc.vector.tensor_copy, w3_bf, 88, P, w3_hi, 64)
+        round_weight(nc.scalar.copy, w3_bf, w3_raw, 0, 44)
+        round_weight(nc.vector.tensor_copy, w3_bf, w3_raw, 44, P)
+        eq_w = placed(raw_room, 0, "eq_w", [P, N], U32)
+        pick(eq_w, e_w[:].bitcast(U32), obs_l)
+        eq = (eq_w, eq_s)
+        rad_g = placed(raw_room, 4096, "rad_g", [P, N], F32)
+        nc.scalar.activation(rad_g[:], rad_t[:].indirect(obs_l[:]), ACT.Copy)
         w3q = quantize_whole("w3q", w3_bf)
         obst = sb("obst", [P, PACK, N], F32)
         for t in range(PACK):
@@ -165,16 +163,18 @@ def tile_picked_ycollid_pen_p_kernel(
 
         xq_w = placed(w3_room, 0, "xq_w", [P, N], U32)
         xq_s = placed(w3_room, 2048, "xq_s", [P, N], U8)
-        xq = pick(xq_w, xq_s, x_w, x_s, offs_l)
+        pick(xq_w, x_w[:].bitcast(U32), offs_l)
+        pick(xq_s, x_s[:], offs_l)
+        xq = (xq_w, xq_s)
         w2_bf = sb("w2_bf", [P, PACK * N], BF16, "x_s_then_w2")
-        round_weight(nc.vector.tensor_copy, w2_bf, 0, P, w2_raw)
+        round_weight(nc.vector.tensor_copy, w2_bf, w2_raw, 0, P)
         hid2_planes = sb("hid2_planes", [P, PACK, N], F32, "w2_then_hid2")
 
         def scale_obst(t):
             nc.vector.tensor_scalar(hid2_planes[:, t, :], obst[:, t, :], unit2_t[:, t : t + 1], None, ALU.mult)
 
-        def weave(name, planes):
-            g = sb(name, [P, PACK * planes.shape[2]], BF16)
+        def weave(name, planes, tag=None):
+            g = sb(name, [P, PACK * planes.shape[2]], BF16, tag)
             nc.vector.tensor_copy(
                 g[:].rearrange("p (c i t) -> p c t i", i=4, t=PACK),
                 planes.rearrange("p t (c i) -> p c t i", i=4),
@@ -183,20 +183,19 @@ def tile_picked_ycollid_pen_p_kernel(
 
         scale_obst(0)
         w2q = quantize_whole("w2q", w2_bf)
-        w1_bf = sb("w1_bf", [P, PACK * N], BF16, "eq_w_then_w1")
-        round_weight(nc.scalar.copy, w1_bf, 0, 64, w1_lo)
-        rad_g = sb("rad_g", [P, N], F32, "eq_s_then_rad")
-        nc.scalar.activation(rad_g[:], rad_t[:].indirect(obs_l[:]), ACT.Copy, scale=0.5)
+        reach = sb("reach", [P, N], F32, "eq_s_then_reach")
+        nc.scalar.activation(reach[:], rad_g[:], ACT.Exp, scale=2.0, bias=-0.2)
         yv = []
         for t in range(PACK):
             acc = bank(t)
             mm(acc[:], w2q, block(t), xq, slice(0, N))
-            v = sb(f"yv{t}", [P, N], F32, "yv_then_reach" if t == 3 else None)
+            v = sb(f"yv{t}", [P, N], F32)
             nc.scalar.activation(v[:], acc[:], ACT.Copy, scale=unit_par[:, t : t + 1])
             yv.append(v)
         scale_obst(1)
         scale_obst(2)
-        round_weight(nc.vector.tensor_copy, w1_bf, 64, P, w1_hi, 64)
+        w1_bf = placed(raw_room, 0, "w1_bf", [P, PACK * N], BF16)
+        round_weight(nc.vector.tensor_copy, w1_bf, w1_raw, 0, P)
         scale_obst(3)
         w1q = quantize_whole("w1q", w1_bf)
         y = []
@@ -216,50 +215,46 @@ def tile_picked_ycollid_pen_p_kernel(
             )
 
         def quantize_half(h):
-            woven = [weave(f"hid{2 * h + u}", planes[h][:, :, block(u)]) for u in range(2)]
+            woven = [
+                weave(f"hid{2 * h + u}", planes[h][:, :, block(u)], "hid_then_expo" if 2 * h + u == 3 else None)
+                for u in range(2)
+            ]
             return [quantize_whole(f"hidq{2 * h + u}", woven[u]) for u in range(2)]
+
+        def parents(h, t):
+            return yv[t][:].indirect(par_l[:, block(h, LIST_HALF)])
 
         for h in range(2):
             for t in range(PACK):
-                nc.scalar.activation(vp[h][t][:], yv[t][:].indirect(par_l[:, block(h, LIST_HALF)]), ACT.Copy)
-        reach = sb("reach", [P, N], F32, "yv_then_reach")
-        nc.scalar.activation(reach[:], rad_g[:], ACT.Exp, scale=4.0, bias=-0.2)
+                nc.scalar.activation(vp[h][t][:], parents(h, t), ACT.Copy)
         join(0, 0)
-        join(0, 1)
         hid2q = quantize_whole("hid2q", hid2)
-        join(0, 2)
-        join(0, 3)
+        for t in range(1, PACK):
+            join(0, t)
         hidq = quantize_half(0)
         for t in range(PACK):
             join(1, t)
         hidq = hidq + quantize_half(1)
 
-        expo = []
-        for r in range(2):
+        mag0 = sb("mag0", [P, N], F32)
+        later = placed(pen_room, 1024, "later", [P, 3, N], F32)
+        decay = []
+        for r in range(4):
             sc = bank(r)
             mm(sc[:], hidq[r], slice(0, P), hid2q, slice(0, N))
-            mag = sb(f"mag{r}", [P, N], F32)
-            nc.scalar.activation(mag[:], sc[:], ACT.Abs)
-            decay = sb(f"decay{r}", [P, N], F32)
-            nc.scalar.activation(decay[:], mag[:], ACT.Exp, scale=-2.0)
-            e = sb(f"expo{r}", [P, N], F32)
-            nc.vector.tensor_tensor(e[:], decay[:], reach[:], ALU.mult)
-            expo.append(e)
-        half_clr = placed(pen_room, 1024, "half_clr", [P, 2, N], F32)
-        for r in range(2, 4):
-            sc = bank(r)
-            mm(sc[:], hidq[r], slice(0, P), hid2q, slice(0, N))
-            part = sb(f"part{r}", [P, N], F32)
-            nc.vector.scalar_tensor_tensor(part[:], sc[:], 0.5, rad_g[:], ALU.mult, ALU.add)
-            nc.vector.scalar_tensor_tensor(half_clr[:, r - 2, :], sc[:], 0.0, part[:], ALU.max, ALU.subtract)
-            e = sb(f"expo{r}", [P, N], F32)
-            nc.scalar.activation(e[:], half_clr[:, r - 2, :], ACT.Exp, scale=-4.0, bias=-0.2)
-            expo.append(e)
+            mag = mag0[:] if r == 0 else later[:, r - 1, :]
+            nc.scalar.activation(mag, sc[:], ACT.Abs)
+            e = sb(f"decay{r}", [P, N], F32)
+            nc.scalar.activation(e[:], mag, ACT.Exp, scale=-2.0)
+            decay.append(e)
+        expo = sb("expo", [P, 4, N], F32, "hid_then_expo")
+        for r in range(4):
+            nc.vector.tensor_tensor(expo[:, r, :], decay[r][:], reach[:], ALU.mult)
 
         pen = []
         for r in range(4):
             p = placed(pen_room, r * N * 4, f"pen{r}", [P, N], F32)
-            nc.scalar.activation(p[:], expo[r][:], ACT.Ln, bias=1.0)
+            nc.scalar.activation(p[:], expo[:, r, :], ACT.Ln, bias=1.0)
             pen.append(p)
 
         for r in range(4):

@@ -29,8 +29,8 @@ def tile_picked_ycollid_pen_p_kernel(
     nc = tc.nc
     with ExitStack() as ctx:
         keep = ctx.enter_context(tc.tile_pool(name="keep", bufs=1))
-        w3_room = ctx.enter_context(tc.tile_pool(name="w3_room", bufs=1))
-        raw_room = ctx.enter_context(tc.tile_pool(name="raw_room", bufs=1))
+        w2_room = ctx.enter_context(tc.tile_pool(name="w2_room", bufs=1))
+        expo_room = ctx.enter_context(tc.tile_pool(name="expo_room", bufs=1))
         pen_room = ctx.enter_context(tc.tile_pool(name="pen_room", bufs=1))
         psum = ctx.enter_context(tc.psum_pool(name="psum", bufs=1))
 
@@ -75,14 +75,14 @@ def tile_picked_ycollid_pen_p_kernel(
         def as_loaded(raw):
             return raw[:].rearrange("p j (m t) -> p m j t", t=PACK)
 
-        def round_weight(copy, g, raw, first, last):
-            copy(dealt(g)[:, first:last], as_loaded(raw)[:, first:last])
+        def round_weight(g, raw):
+            nc.vector.tensor_copy(dealt(g), as_loaded(raw))
 
         def quantize(codes, scales, src):
             nc.vector.quantize_mx(out=codes.bitcast(FP8X4), scales=scales, in_=src)
 
-        def quantize_whole(name, g):
-            c = sb(name + "_c", [P, g.shape[1] // PACK], U32)
+        def quantize_whole(name, g, tag=None):
+            c = sb(name + "_c", [P, g.shape[1] // PACK], U32, tag)
             s = sb(name + "_s", [P, g.shape[1] // PACK], U8)
             quantize(c[:], s[:], g[:])
             return c, s
@@ -102,11 +102,11 @@ def tile_picked_ycollid_pen_p_kernel(
             return slice(i * width, (i + 1) * width)
 
         obs_l = load_list("obs_l", obs_)
-        rad_cols = placed(w3_room, 0, "rad_cols", [P, TABLE // P], F32)
+        rad_cols = sb("rad_cols", [P, TABLE // P], F32)
         nc.scalar.dma_start(rad_cols[:], rad[0, :].rearrange("(p m) -> p m", p=P))
         e_s_rows = sb("e_s_rows", [P, TABLE], U8)
         load_scales(e_s_rows, e_scales)
-        w3_raw = placed(raw_room, 0, "w3_raw", [P, PACK, N], F32)
+        w3_raw = sb("w3_raw", [P, PACK, N], F32, "w3_then_eq_w")
         load_weight(w3_raw, w3)
         e_w = sb("e_w", [P, TABLE], I32)
         load_words(e_w, e_words)
@@ -115,13 +115,13 @@ def tile_picked_ycollid_pen_p_kernel(
         nc.vector.memset(e_s[:].bitcast(I32), 0)
         for q in range(4):
             nc.vector.tensor_copy(scale_rows(e_s, q), scale_rows(e_s_rows, q))
-        x_w = sb("x_w", [P, TABLE], I32)
-        load_words(x_w, x_words)
-        x_s = sb("x_s", [P, TABLE], U8, "x_s_then_w2")
+        x_s = sb("x_s", [P, TABLE], U8)
         nc.vector.memset(x_s[:].bitcast(I32), 0)
         load_scales(x_s, x_scales)
-        w2_raw = sb("w2_raw", [P, PACK, N], F32, "w2_then_hid2")
+        w2_raw = placed(w2_room, 0, "w2_raw", [P, PACK, N], F32)
         load_weight(w2_raw, w2)
+        x_w = sb("x_w", [P, TABLE], I32)
+        load_words(x_w, x_words)
         w1_raw = sb("w1_raw", [P, PACK, N], F32)
         load_weight(w1_raw, w1)
         par_l = load_list("par_l", par)
@@ -144,47 +144,52 @@ def tile_picked_ycollid_pen_p_kernel(
         unit_par = sb("unit_par", [P, PACK], F32)
         nc.gpsimd.tensor_scalar(unit_par[:], unit_t[:], 0.6, 0.0, ALU.mult, ALU.add)
 
-        eq_s = sb("eq_s", [P, N], U8, "eq_s_then_reach")
+        reach = sb("reach", [P, N], F32)
+
+        def make_reach(name, tag, first, last):
+            picked = sb(name, [P, last - first], F32, tag)
+            nc.scalar.activation(picked[:], rad_t[:].indirect(obs_l[:, first // 16 : last // 16]), ACT.Copy)
+            nc.scalar.activation(reach[:, first:last], picked[:], ACT.Exp, scale=2.0, bias=-0.2)
+
+        make_reach("rad_early", "rad_then_w3q", 0, 448)
+
+        eq_s = sb("eq_s", [P, N], U8, "eq_s_then_rad")
         pick(eq_s, e_s[:], obs_l)
-        w3_bf = placed(w3_room, 0, "w3_bf", [P, PACK * N], BF16)
-        round_weight(nc.scalar.copy, w3_bf, w3_raw, 0, 44)
-        round_weight(nc.vector.tensor_copy, w3_bf, w3_raw, 44, P)
-        eq_w = placed(raw_room, 0, "eq_w", [P, N], U32)
+        w3_bf = sb("w3_bf", [P, PACK * N], BF16, "rounded")
+        round_weight(w3_bf, w3_raw)
+        eq_w = sb("eq_w", [P, N], U32, "w3_then_eq_w")
         pick(eq_w, e_w[:].bitcast(U32), obs_l)
         eq = (eq_w, eq_s)
-        rad_g = placed(raw_room, 4096, "rad_g", [P, N], F32)
-        nc.scalar.activation(rad_g[:], rad_t[:].indirect(obs_l[:]), ACT.Copy)
-        w3q = quantize_whole("w3q", w3_bf)
+        w3q = quantize_whole("w3q", w3_bf, "rad_then_w3q")
         obst = sb("obst", [P, PACK, N], F32)
         for t in range(PACK):
             ye = bank(4 + t)
             mm(ye[:], w3q, block(t), eq, slice(0, N))
             nc.scalar.activation(obst[:, t, :], ye[:], ACT.Gelu_apprx_tanh)
+        make_reach("rad_late", "eq_s_then_rad", 448, N)
 
-        xq_w = placed(w3_room, 0, "xq_w", [P, N], U32)
-        xq_s = placed(w3_room, 2048, "xq_s", [P, N], U8)
-        pick(xq_w, x_w[:].bitcast(U32), offs_l)
+        w2_bf = sb("w2_bf", [P, PACK * N], BF16, "rounded")
+        round_weight(w2_bf, w2_raw)
+        xq_w = placed(w2_room, 0, "xq_w", [P, N], U32)
+        xq_s = placed(w2_room, 2048, "xq_s", [P, N], U8)
         pick(xq_s, x_s[:], offs_l)
+        pick(xq_w, x_w[:].bitcast(U32), offs_l)
         xq = (xq_w, xq_s)
-        w2_bf = sb("w2_bf", [P, PACK * N], BF16, "x_s_then_w2")
-        round_weight(nc.vector.tensor_copy, w2_bf, w2_raw, 0, P)
-        hid2_planes = sb("hid2_planes", [P, PACK, N], F32, "w2_then_hid2")
+        hid2_planes = sb("hid2_planes", [P, PACK, N], F32)
 
-        def scale_obst(t):
-            nc.vector.tensor_scalar(hid2_planes[:, t, :], obst[:, t, :], unit2_t[:, t : t + 1], None, ALU.mult)
+        def scale_obst(engine, t):
+            engine.tensor_scalar(hid2_planes[:, t, :], obst[:, t, :], unit2_t[:, t : t + 1], 0.0, ALU.mult, ALU.add)
 
-        def weave(name, planes, tag=None):
-            g = sb(name, [P, PACK * planes.shape[2]], BF16, tag)
+        def weave(g, planes):
             nc.vector.tensor_copy(
                 g[:].rearrange("p (c i t) -> p c t i", i=4, t=PACK),
                 planes.rearrange("p t (c i) -> p c t i", i=4),
             )
             return g
 
-        scale_obst(0)
+        for t in range(3):
+            scale_obst(nc.gpsimd, t)
         w2q = quantize_whole("w2q", w2_bf)
-        reach = sb("reach", [P, N], F32, "eq_s_then_reach")
-        nc.scalar.activation(reach[:], rad_g[:], ACT.Exp, scale=2.0, bias=-0.2)
         yv = []
         for t in range(PACK):
             acc = bank(t)
@@ -192,33 +197,32 @@ def tile_picked_ycollid_pen_p_kernel(
             v = sb(f"yv{t}", [P, N], F32)
             nc.scalar.activation(v[:], acc[:], ACT.Copy, scale=unit_par[:, t : t + 1])
             yv.append(v)
-        scale_obst(1)
-        scale_obst(2)
-        w1_bf = placed(raw_room, 0, "w1_bf", [P, PACK * N], BF16)
-        round_weight(nc.vector.tensor_copy, w1_bf, w1_raw, 0, P)
-        scale_obst(3)
+        w1_bf = sb("w1_bf", [P, PACK * N], BF16, "rounded")
+        round_weight(w1_bf, w1_raw)
+        scale_obst(nc.vector, 3)
         w1q = quantize_whole("w1q", w1_bf)
         y = []
         for t in range(PACK):
             acc = bank(4 + t)
             mm(acc[:], w1q, block(t), xq, slice(0, N))
             y.append(acc)
-        hid2 = weave("hid2", hid2_planes[:])
+        hid2 = weave(sb("hid2", [P, PACK * N], BF16, "hid2_then_planes"), hid2_planes[:])
 
         vp = [[sb(f"vp{h}_{t}", [P, HALF], F32) for t in range(PACK)] for h in range(2)]
 
-        planes = [sb(f"hid_planes{h}", [P, PACK, HALF], F32) for h in range(2)]
+        hid2q = quantize_whole("hid2q", hid2)
+        planes = [sb("hid_planes0", [P, PACK, HALF], F32, "hid2_then_planes")]
 
         def join(h, t):
             nc.vector.scalar_tensor_tensor(
                 planes[h][:, t, :], y[t][:, block(h, HALF)], unit_t[:, t : t + 1], vp[h][t][:], ALU.mult, ALU.add
             )
 
+        hid = [sb(f"hid{r}", [P, PACK * P], BF16, "hid_then_planes" if r == 0 else None) for r in range(3)]
+        hid.append(placed(expo_room, 3584, "hid3", [P, PACK * P], BF16))
+
         def quantize_half(h):
-            woven = [
-                weave(f"hid{2 * h + u}", planes[h][:, :, block(u)], "hid_then_expo" if 2 * h + u == 3 else None)
-                for u in range(2)
-            ]
+            woven = [weave(hid[2 * h + u], planes[h][:, :, block(u)]) for u in range(2)]
             return [quantize_whole(f"hidq{2 * h + u}", woven[u]) for u in range(2)]
 
         def parents(h, t):
@@ -227,17 +231,16 @@ def tile_picked_ycollid_pen_p_kernel(
         for h in range(2):
             for t in range(PACK):
                 nc.scalar.activation(vp[h][t][:], parents(h, t), ACT.Copy)
-        join(0, 0)
-        hid2q = quantize_whole("hid2q", hid2)
-        for t in range(1, PACK):
+        for t in range(PACK):
             join(0, t)
         hidq = quantize_half(0)
+        planes.append(sb("hid_planes1", [P, PACK, HALF], F32, "hid_then_planes"))
         for t in range(PACK):
             join(1, t)
         hidq = hidq + quantize_half(1)
 
         mag0 = sb("mag0", [P, N], F32)
-        later = placed(pen_room, 1024, "later", [P, 3, N], F32)
+        later = placed(pen_room, 3072, "later", [P, 3, N], F32)
         decay = []
         for r in range(4):
             sc = bank(r)
@@ -247,35 +250,41 @@ def tile_picked_ycollid_pen_p_kernel(
             e = sb(f"decay{r}", [P, N], F32)
             nc.scalar.activation(e[:], mag, ACT.Exp, scale=-2.0)
             decay.append(e)
-        expo = sb("expo", [P, 4, N], F32, "hid_then_expo")
-        for r in range(4):
-            nc.vector.tensor_tensor(expo[:, r, :], decay[r][:], reach[:], ALU.mult)
 
-        pen = []
-        for r in range(4):
-            p = placed(pen_room, r * N * 4, f"pen{r}", [P, N], F32)
-            nc.scalar.activation(p[:], expo[:, r, :], ACT.Ln, bias=1.0)
-            pen.append(p)
+        def next_of(window, h):
+            return window.indirect(nxo_l[:, block(h, LIST_HALF)])
 
+        expo = []
         for r in range(4):
-            res = sb(f"res{r}", [P, N], F32)
             if r < 2:
-                half_pen = sb(f"half_pen{r}", [P, N], F32)
-                nc.vector.tensor_scalar(half_pen[:], pen[r][:], 0.5, None, ALU.mult)
+                both = placed(expo_room, r * 4096, f"both{r}", [P, 2 * N], F32)
+                nc.vector.tensor_tensor(both[:, 0:N], decay[r][:], reach[:], ALU.mult)
                 for h in range(2):
-                    nc.vector.tensor_tensor(
-                        res[:, block(h, HALF)],
-                        half_pen[:].indirect(nxo_l[:, block(h, LIST_HALF)]),
-                        pen[r][:, block(h, HALF)],
-                        ALU.add,
-                    )
-                nc.sync.dma_start(out[block(r), :], res[:])
+                    nc.vector.tensor_copy(both[:, block(2 + h, HALF)], next_of(both[:, 0:N], h))
+                expo.append(both)
             else:
-                nxt = sb(f"next{r}", [P, N], F32)
-                for h in range(2):
-                    cols = block(h, HALF)
-                    nc.scalar.activation(nxt[:, cols], pen[r][:].indirect(nxo_l[:, block(h, LIST_HALF)]), ACT.Copy)
-                    nc.vector.scalar_tensor_tensor(
-                        res[:, cols], nxt[:, cols], 0.5, pen[r][:, cols], ALU.mult, ALU.add
-                    )
-                    nc.sync.dma_start(out[block(r), cols], res[:, cols])
+                e = sb(f"expo{r}", [P, N], F32)
+                nc.vector.tensor_tensor(e[:], decay[r][:], reach[:], ALU.mult)
+                expo.append(e)
+
+        pen = {}
+        for r, offset in ((2, 4096), (0, 0), (3, 6144), (1, 8192)):
+            pen[r] = placed(pen_room, offset, f"pen{r}", list(expo[r].shape), F32)
+            nc.scalar.activation(pen[r][:], expo[r][:], ACT.Ln, bias=1.0)
+
+        res = [sb(f"res{r}", [P, N], F32) for r in range(4)]
+        half_pen = sb("half_pen", [P, N], F32)
+        nc.vector.tensor_scalar(half_pen[:], pen[2][:], 0.5, None, ALU.mult)
+        for h in range(2):
+            cols = block(h, HALF)
+            nc.vector.tensor_tensor(res[2][:, cols], next_of(half_pen[:], h), pen[2][:, cols], ALU.add)
+        nc.sync.dma_start(out[block(2), :], res[2][:])
+        for r in range(2):
+            nc.vector.scalar_tensor_tensor(res[r][:], pen[r][:, N : 2 * N], 0.5, pen[r][:, 0:N], ALU.mult, ALU.add)
+            nc.sync.dma_start(out[block(r), :], res[r][:])
+        nxt = sb("next3", [P, N], F32)
+        for h in range(2):
+            cols = block(h, HALF)
+            nc.scalar.activation(nxt[:, cols], next_of(pen[3][:], h), ACT.Copy)
+            nc.vector.scalar_tensor_tensor(res[3][:, cols], nxt[:, cols], 0.5, pen[3][:, cols], ALU.mult, ALU.add)
+            nc.sync.dma_start(out[block(3), cols], res[3][:, cols])

@@ -17,8 +17,16 @@ P = 128
 PACK = 4
 N = 512
 TABLE = 1024
+TILES = N // P
 HALF = N // 2
-LIST_HALF = HALF // 16
+PER_COLUMN = 16
+QUADRANT = 32
+RUN = 4
+RAD_PER_PARTITION = TABLE // P
+LATE = 64
+EARLY = N - LATE
+PRE = 2
+F32_TILE = N * 4
 
 FLOPS = 4 * 2 * N * N * N
 
@@ -43,8 +51,14 @@ def tile_picked_ycollid_pen_p_kernel(
         def bank(b):
             return psum.tile([P, N], F32, name=f"bank{b}")
 
+        def block(i, width=P):
+            return slice(i * width, (i + 1) * width)
+
+        def entries(lst, first, last):
+            return lst[:, first // PER_COLUMN : last // PER_COLUMN]
+
         def load_list(name, src):
-            t = sb(name, [P, N // 16], U16)
+            t = sb(name, [P, N // PER_COLUMN], U16)
             nc.sync.dma_start(t[:], src)
             return t
 
@@ -52,11 +66,11 @@ def tile_picked_ycollid_pen_p_kernel(
             nc.sync.dma_start(t[:], words[0].rearrange("p c r -> p (c r)").bitcast(I32))
 
         def scale_rows(t, q):
-            return t[32 * q : 32 * q + 4, :].bitcast(I32)
+            return t[QUADRANT * q : QUADRANT * q + PACK, :].bitcast(I32)
 
         def load_scales(t, scales):
-            for q in range(4):
-                nc.sync.dma_start(scale_rows(t, q), scales[0, 4 * q : 4 * q + 4, :].bitcast(I32))
+            for q in range(P // QUADRANT):
+                nc.sync.dma_start(scale_rows(t, q), scales[0, PACK * q : PACK * q + PACK, :].bitcast(I32))
 
         def load_weight(t, w):
             nc.sync.dma_start(t[:], w.rearrange("(p j) c -> p j c", j=PACK))
@@ -69,40 +83,38 @@ def tile_picked_ycollid_pen_p_kernel(
         def pick(picked, table, lst):
             nc.vector.tensor_copy(picked[:], table.indirect(lst[:]))
 
-        def dealt(g):
-            return g[:].rearrange("p (t m j) -> p m j t", t=PACK, j=PACK)
+        def round_weight(rounded, raw):
+            nc.vector.tensor_copy(
+                rounded[:].rearrange("p (t m j) -> p m j t", t=PACK, j=PACK),
+                raw[:].rearrange("p j (m t) -> p m j t", t=PACK),
+            )
 
-        def as_loaded(raw):
-            return raw[:].rearrange("p j (m t) -> p m j t", t=PACK)
+        def weave(woven, planes):
+            nc.vector.tensor_copy(
+                woven[:].rearrange("p (c i t) -> p c t i", i=RUN, t=PACK),
+                planes.rearrange("p t (c i) -> p c t i", i=RUN),
+            )
+            return woven
 
-        def round_weight(g, raw):
-            nc.vector.tensor_copy(dealt(g), as_loaded(raw))
+        def quantize(name, values, tag=None):
+            codes = sb(name + "_codes", [P, values.shape[1] // PACK], U32, tag)
+            scales = sb(name + "_scales", [P, values.shape[1] // PACK], U8)
+            nc.vector.quantize_mx(out=codes[:].bitcast(FP8X4), scales=scales[:], in_=values[:])
+            return codes, scales
 
-        def quantize(codes, scales, src):
-            nc.vector.quantize_mx(out=codes.bitcast(FP8X4), scales=scales, in_=src)
-
-        def quantize_whole(name, g, tag=None):
-            c = sb(name + "_c", [P, g.shape[1] // PACK], U32, tag)
-            s = sb(name + "_s", [P, g.shape[1] // PACK], U8)
-            quantize(c[:], s[:], g[:])
-            return c, s
-
-        def mm(dst, lhs, lcols, rhs, rcols):
+        def product(acc, lhs, cols, rhs):
             nc.tensor.matmul_mx(
-                out=dst,
-                lhsT=lhs[0][:, lcols].bitcast(FP8X4),
-                lhsT_scale=lhs[1][:, lcols],
-                rhs=rhs[0][:, rcols].bitcast(FP8X4),
-                rhs_scale=rhs[1][:, rcols],
+                out=acc[:],
+                lhsT=lhs[0][:, cols].bitcast(FP8X4),
+                lhsT_scale=lhs[1][:, cols],
+                rhs=rhs[0][:].bitcast(FP8X4),
+                rhs_scale=rhs[1][:],
                 start=True,
                 stop=True,
             )
 
-        def block(i, width=P):
-            return slice(i * width, (i + 1) * width)
-
         obs_l = load_list("obs_l", obs_)
-        rad_cols = sb("rad_cols", [P, TABLE // P], F32)
+        rad_cols = sb("rad_cols", [P, RAD_PER_PARTITION], F32)
         nc.scalar.dma_start(rad_cols[:], rad[0, :].rearrange("(p m) -> p m", p=P))
         e_s_rows = sb("e_s_rows", [P, TABLE], U8)
         load_scales(e_s_rows, e_scales)
@@ -113,7 +125,7 @@ def tile_picked_ycollid_pen_p_kernel(
         offs_l = load_list("offs_l", offs)
         e_s = sb("e_s", [P, TABLE], U8)
         nc.vector.memset(e_s[:].bitcast(I32), 0)
-        for q in range(4):
+        for q in range(P // QUADRANT):
             nc.vector.tensor_copy(scale_rows(e_s, q), scale_rows(e_s_rows, q))
         x_s = sb("x_s", [P, TABLE], U8)
         nc.vector.memset(x_s[:].bitcast(I32), 0)
@@ -132,26 +144,29 @@ def tile_picked_ycollid_pen_p_kernel(
         unit_t = load_unit("unit_t", unit)
 
         rad_t = sb("rad_t", [P, TABLE], F32)
-        for b in range(2):
+        for b in range(RAD_PER_PARTITION // TILES):
             spread = bank(b)
-            for m in range(4):
-                col = rad_cols[:, 4 * b + m : 4 * b + m + 1]
+            for m in range(TILES):
+                col = rad_cols[:, TILES * b + m : TILES * b + m + 1]
                 nc.tensor.transpose(spread[:, block(m)], col.to_broadcast([P, P]), ident[:])
             nc.scalar.copy(
-                rad_t[:].rearrange("p (n m) -> p n m", m=8)[:, :, 4 * b : 4 * b + 4],
-                spread[:].rearrange("p (m n) -> p n m", m=4),
+                rad_t[:].rearrange("p (n m) -> p n m", m=RAD_PER_PARTITION)[:, :, block(b, TILES)],
+                spread[:].rearrange("p (m n) -> p n m", m=TILES),
             )
         unit_par = sb("unit_par", [P, PACK], F32)
         nc.gpsimd.tensor_scalar(unit_par[:], unit_t[:], 0.6, 0.0, ALU.mult, ALU.add)
 
         reach = sb("reach", [P, N], F32)
 
-        def make_reach(name, tag, first, last):
+        def fetch_radius(name, tag, first, last):
             picked = sb(name, [P, last - first], F32, tag)
-            nc.scalar.activation(picked[:], rad_t[:].indirect(obs_l[:, first // 16 : last // 16]), ACT.Copy)
+            nc.scalar.activation(picked[:], rad_t[:].indirect(entries(obs_l, first, last)), ACT.Copy)
+            return picked
+
+        def make_reach(picked, first, last):
             nc.scalar.activation(reach[:, first:last], picked[:], ACT.Exp, scale=2.0, bias=-0.2)
 
-        make_reach("rad_early", "rad_then_w3q", 0, 448)
+        make_reach(fetch_radius("rad_early", "rad_then_w3q", 0, EARLY), 0, EARLY)
 
         eq_s = sb("eq_s", [P, N], U8, "eq_s_then_rad")
         pick(eq_s, e_s[:], obs_l)
@@ -160,128 +175,117 @@ def tile_picked_ycollid_pen_p_kernel(
         eq_w = sb("eq_w", [P, N], U32, "w3_then_eq_w")
         pick(eq_w, e_w[:].bitcast(U32), obs_l)
         eq = (eq_w, eq_s)
-        w3q = quantize_whole("w3q", w3_bf, "rad_then_w3q")
+        w3q = quantize("w3q", w3_bf, "rad_then_w3q")
         obst = sb("obst", [P, PACK, N], F32)
         for t in range(PACK):
-            ye = bank(4 + t)
-            mm(ye[:], w3q, block(t), eq, slice(0, N))
+            ye = bank(PACK + t)
+            product(ye, w3q, block(t), eq)
+            if t == PACK - 1:
+                rad_late = fetch_radius("rad_late", "eq_s_then_rad", EARLY, N)
             nc.scalar.activation(obst[:, t, :], ye[:], ACT.Gelu_apprx_tanh)
-        make_reach("rad_late", "eq_s_then_rad", 448, N)
+        make_reach(rad_late, EARLY, N)
 
         w2_bf = sb("w2_bf", [P, PACK * N], BF16, "rounded")
         round_weight(w2_bf, w2_raw)
         xq_w = placed(w2_room, 0, "xq_w", [P, N], U32)
-        xq_s = placed(w2_room, 2048, "xq_s", [P, N], U8)
+        xq_s = placed(w2_room, F32_TILE, "xq_s", [P, N], U8)
         pick(xq_s, x_s[:], offs_l)
         pick(xq_w, x_w[:].bitcast(U32), offs_l)
         xq = (xq_w, xq_s)
+
         hid2_planes = sb("hid2_planes", [P, PACK, N], F32)
 
         def scale_obst(engine, t):
             engine.tensor_scalar(hid2_planes[:, t, :], obst[:, t, :], unit2_t[:, t : t + 1], 0.0, ALU.mult, ALU.add)
 
-        def weave(g, planes):
-            nc.vector.tensor_copy(
-                g[:].rearrange("p (c i t) -> p c t i", i=4, t=PACK),
-                planes.rearrange("p t (c i) -> p c t i", i=4),
-            )
-            return g
-
-        for t in range(3):
+        for t in range(PACK - 1):
             scale_obst(nc.gpsimd, t)
-        w2q = quantize_whole("w2q", w2_bf)
+        w2q = quantize("w2q", w2_bf)
         yv = []
         for t in range(PACK):
             acc = bank(t)
-            mm(acc[:], w2q, block(t), xq, slice(0, N))
-            v = sb(f"yv{t}", [P, N], F32)
-            nc.scalar.activation(v[:], acc[:], ACT.Copy, scale=unit_par[:, t : t + 1])
-            yv.append(v)
+            product(acc, w2q, block(t), xq)
+            window = sb(f"yv{t}", [P, N], F32)
+            nc.scalar.activation(window[:], acc[:], ACT.Copy, scale=unit_par[:, t : t + 1])
+            yv.append(window)
         w1_bf = sb("w1_bf", [P, PACK * N], BF16, "rounded")
         round_weight(w1_bf, w1_raw)
-        scale_obst(nc.vector, 3)
-        w1q = quantize_whole("w1q", w1_bf)
+        scale_obst(nc.vector, PACK - 1)
+        w1q = quantize("w1q", w1_bf)
         y = []
         for t in range(PACK):
-            acc = bank(4 + t)
-            mm(acc[:], w1q, block(t), xq, slice(0, N))
+            acc = bank(PACK + t)
+            product(acc, w1q, block(t), xq)
             y.append(acc)
         hid2 = weave(sb("hid2", [P, PACK * N], BF16, "hid2_then_planes"), hid2_planes[:])
+        hid2q = quantize("hid2q", hid2)
 
         vp = [[sb(f"vp{h}_{t}", [P, HALF], F32) for t in range(PACK)] for h in range(2)]
-
-        hid2q = quantize_whole("hid2q", hid2)
-        planes = [sb("hid_planes0", [P, PACK, HALF], F32, "hid2_then_planes")]
-
-        def join(h, t):
-            nc.vector.scalar_tensor_tensor(
-                planes[h][:, t, :], y[t][:, block(h, HALF)], unit_t[:, t : t + 1], vp[h][t][:], ALU.mult, ALU.add
-            )
-
-        hid = [sb(f"hid{r}", [P, PACK * P], BF16, "hid_then_planes" if r == 0 else None) for r in range(3)]
-        hid.append(placed(expo_room, 3584, "hid3", [P, PACK * P], BF16))
-
-        def quantize_half(h):
-            woven = [weave(hid[2 * h + u], planes[h][:, :, block(u)]) for u in range(2)]
-            return [quantize_whole(f"hidq{2 * h + u}", woven[u]) for u in range(2)]
-
-        def parents(h, t):
-            return yv[t][:].indirect(par_l[:, block(h, LIST_HALF)])
-
         for h in range(2):
             for t in range(PACK):
-                nc.scalar.activation(vp[h][t][:], parents(h, t), ACT.Copy)
-        for t in range(PACK):
-            join(0, t)
-        hidq = quantize_half(0)
-        planes.append(sb("hid_planes1", [P, PACK, HALF], F32, "hid_then_planes"))
-        for t in range(PACK):
-            join(1, t)
-        hidq = hidq + quantize_half(1)
+                parents = yv[t][:].indirect(entries(par_l, h * HALF, (h + 1) * HALF))
+                nc.scalar.activation(vp[h][t][:], parents, ACT.Copy)
 
-        mag0 = sb("mag0", [P, N], F32)
-        later = placed(pen_room, 3072, "later", [P, 3, N], F32)
+        hid = [sb(f"hid{r}", [P, PACK * P], BF16, "hid_then_planes" if r == 0 else None) for r in range(TILES - 1)]
+        hid.append(placed(expo_room, 2 * F32_TILE - PACK * P, f"hid{TILES - 1}", [P, PACK * P], BF16))
+        hidq = []
+        for h, tag in enumerate(("hid2_then_planes", "hid_then_planes")):
+            planes = sb(f"hid_planes{h}", [P, PACK, HALF], F32, tag)
+            for t in range(PACK):
+                nc.vector.scalar_tensor_tensor(
+                    planes[:, t, :], y[t][:, block(h, HALF)], unit_t[:, t : t + 1], vp[h][t][:], ALU.mult, ALU.add
+                )
+            woven = [weave(hid[2 * h + u], planes[:, :, block(u)]) for u in range(2)]
+            hidq.extend([quantize(f"hidq{2 * h + u}", woven[u]) for u in range(2)])
+
+        first_mag = sb("first_mag", [P, N], F32)
+        later_mags = placed(pen_room, 3 * F32_TILE // 2, "later_mags", [P, TILES - 1, N], F32)
         decay = []
-        for r in range(4):
+        for r in range(TILES):
             sc = bank(r)
-            mm(sc[:], hidq[r], slice(0, P), hid2q, slice(0, N))
-            mag = mag0[:] if r == 0 else later[:, r - 1, :]
+            product(sc, hidq[r], block(0), hid2q)
+            mag = first_mag[:] if r == 0 else later_mags[:, r - 1, :]
             nc.scalar.activation(mag, sc[:], ACT.Abs)
-            e = sb(f"decay{r}", [P, N], F32)
-            nc.scalar.activation(e[:], mag, ACT.Exp, scale=-2.0)
-            decay.append(e)
+            decay.append(sb(f"decay{r}", [P, N], F32))
+            nc.scalar.activation(decay[r][:], mag, ACT.Exp, scale=-2.0)
 
         def next_of(window, h):
-            return window.indirect(nxo_l[:, block(h, LIST_HALF)])
+            return window.indirect(entries(nxo_l, h * HALF, (h + 1) * HALF))
 
         expo = []
-        for r in range(4):
-            if r < 2:
-                both = placed(expo_room, r * 4096, f"both{r}", [P, 2 * N], F32)
+        for r in range(TILES):
+            if r < PRE:
+                both = placed(expo_room, r * 2 * F32_TILE, f"expo{r}", [P, 2 * N], F32)
                 nc.vector.tensor_tensor(both[:, 0:N], decay[r][:], reach[:], ALU.mult)
                 for h in range(2):
                     nc.vector.tensor_copy(both[:, block(2 + h, HALF)], next_of(both[:, 0:N], h))
                 expo.append(both)
             else:
-                e = sb(f"expo{r}", [P, N], F32)
-                nc.vector.tensor_tensor(e[:], decay[r][:], reach[:], ALU.mult)
-                expo.append(e)
+                expo.append(sb(f"expo{r}", [P, N], F32))
+                nc.vector.tensor_tensor(expo[r][:], decay[r][:], reach[:], ALU.mult)
 
         pen = {}
-        for r, offset in ((2, 4096), (0, 0), (3, 6144), (1, 8192)):
-            pen[r] = placed(pen_room, offset, f"pen{r}", list(expo[r].shape), F32)
+        offset = 0
+        for r in (0, 2, 3, 1):
+            width = expo[r].shape[1]
+            pen[r] = placed(pen_room, offset, f"pen{r}", [P, width], F32)
             nc.scalar.activation(pen[r][:], expo[r][:], ACT.Ln, bias=1.0)
+            offset = offset + width * 4
 
-        res = [sb(f"res{r}", [P, N], F32) for r in range(4)]
+        res = [sb(f"res{r}", [P, N], F32) for r in range(TILES)]
+
+        def finish_gathered(r):
+            nc.vector.scalar_tensor_tensor(res[r][:], pen[r][:, N : 2 * N], 0.5, pen[r][:, 0:N], ALU.mult, ALU.add)
+            nc.sync.dma_start(out[block(r), :], res[r][:])
+
+        finish_gathered(0)
         half_pen = sb("half_pen", [P, N], F32)
         nc.vector.tensor_scalar(half_pen[:], pen[2][:], 0.5, None, ALU.mult)
         for h in range(2):
             cols = block(h, HALF)
             nc.vector.tensor_tensor(res[2][:, cols], next_of(half_pen[:], h), pen[2][:, cols], ALU.add)
         nc.sync.dma_start(out[block(2), :], res[2][:])
-        for r in range(2):
-            nc.vector.scalar_tensor_tensor(res[r][:], pen[r][:, N : 2 * N], 0.5, pen[r][:, 0:N], ALU.mult, ALU.add)
-            nc.sync.dma_start(out[block(r), :], res[r][:])
+        finish_gathered(1)
         nxt = sb("next3", [P, N], F32)
         for h in range(2):
             cols = block(h, HALF)

from contextlib import ExitStack

import concourse.mybir as mybir
from concourse.masks import make_identity

F32 = mybir.dt.float32
BF16 = mybir.dt.bfloat16
I32 = mybir.dt.int32
U32 = mybir.dt.uint32
U16 = mybir.dt.uint16
U8 = mybir.dt.uint8
FP8X4 = mybir.dt.float8_e4m3fn_x4
ACT = mybir.ActivationFunctionType
ALU = mybir.AluOpType

P = 128
PACK = 4
N = 512
TABLE = 1024
TILES = N // P
HALF = N // 2
PER_COLUMN = 16
QUADRANT = 32
RUN = 4
RAD_PER_PARTITION = TABLE // P
LATE = 64
EARLY = N - LATE
PRE = 2
F32_TILE = N * 4

FLOPS = 4 * 2 * N * N * N


def tile_picked_ycollid_pen_p_kernel(
    tc, x_words, x_scales, w1, w2, e_words, e_scales, w3, unit, unit2, rad, offs, obs_, par, nxo, out
):
    nc = tc.nc
    with ExitStack() as ctx:
        keep = ctx.enter_context(tc.tile_pool(name="keep", bufs=1))
        w2_room = ctx.enter_context(tc.tile_pool(name="w2_room", bufs=1))
        expo_room = ctx.enter_context(tc.tile_pool(name="expo_room", bufs=1))
        pen_room = ctx.enter_context(tc.tile_pool(name="pen_room", bufs=1))
        psum = ctx.enter_context(tc.psum_pool(name="psum", bufs=1))

        def sb(name, shape, dtype, tag=None):
            return keep.tile(shape, dtype, name=name, tag=tag or name, align_bytes=64)

        def placed(room, offset, name, shape, dtype):
            return room.tile(shape, dtype, name=name, align_bytes=64, offset=offset)

        def bank(b):
            return psum.tile([P, N], F32, name=f"bank{b}")

        def block(i, width=P):
            return slice(i * width, (i + 1) * width)

        def entries(lst, first, last):
            return lst[:, first // PER_COLUMN : last // PER_COLUMN]

        def load_list(name, src):
            t = sb(name, [P, N // PER_COLUMN], U16)
            nc.sync.dma_start(t[:], src)
            return t

        def load_words(t, words):
            nc.sync.dma_start(t[:], words[0].rearrange("p c r -> p (c r)").bitcast(I32))

        def scale_rows(t, q):
            return t[QUADRANT * q : QUADRANT * q + PACK, :].bitcast(I32)

        def load_scales(t, scales):
            for q in range(P // QUADRANT):
                nc.sync.dma_start(scale_rows(t, q), scales[0, PACK * q : PACK * q + PACK, :].bitcast(I32))

        def load_weight(t, w):
            nc.sync.dma_start(t[:], w.rearrange("(p j) c -> p j c", j=PACK))

        def load_unit(name, u):
            t = sb(name, [P, PACK], F32)
            nc.gpsimd.dma_start(t[:], u.rearrange("(p t) o -> p (t o)", t=PACK))
            return t

        def pick(picked, table, lst):
            nc.vector.tensor_copy(picked[:], table.indirect(lst[:]))

        def round_weight(rounded, raw):
            nc.vector.tensor_copy(
                rounded[:].rearrange("p (t m j) -> p m j t", t=PACK, j=PACK),
                raw[:].rearrange("p j (m t) -> p m j t", t=PACK),
            )

        def weave(woven, planes):
            nc.vector.tensor_copy(
                woven[:].rearrange("p (c i t) -> p c t i", i=RUN, t=PACK),
                planes.rearrange("p t (c i) -> p c t i", i=RUN),
            )
            return woven

        def quantize(name, values, tag=None):
            codes = sb(name + "_codes", [P, values.shape[1] // PACK], U32, tag)
            scales = sb(name + "_scales", [P, values.shape[1] // PACK], U8)
            nc.vector.quantize_mx(out=codes[:].bitcast(FP8X4), scales=scales[:], in_=values[:])
            return codes, scales

        def product(acc, lhs, cols, rhs):
            nc.tensor.matmul_mx(
                out=acc[:],
                lhsT=lhs[0][:, cols].bitcast(FP8X4),
                lhsT_scale=lhs[1][:, cols],
                rhs=rhs[0][:].bitcast(FP8X4),
                rhs_scale=rhs[1][:],
                start=True,
                stop=True,
            )

        obs_l = load_list("obs_l", obs_)
        rad_cols = sb("rad_cols", [P, RAD_PER_PARTITION], F32)
        nc.scalar.dma_start(rad_cols[:], rad[0, :].rearrange("(p m) -> p m", p=P))
        e_s_rows = sb("e_s_rows", [P, TABLE], U8)
        load_scales(e_s_rows, e_scales)
        w3_raw = sb("w3_raw", [P, PACK, N], F32, "w3_then_eq_w")
        load_weight(w3_raw, w3)
        e_w = sb("e_w", [P, TABLE], I32)
        load_words(e_w, e_words)
        offs_l = load_list("offs_l", offs)
        e_s = sb("e_s", [P, TABLE], U8)
        nc.vector.memset(e_s[:].bitcast(I32), 0)
        for q in range(P // QUADRANT):
            nc.vector.tensor_copy(scale_rows(e_s, q), scale_rows(e_s_rows, q))
        x_s = sb("x_s", [P, TABLE], U8)
        nc.vector.memset(x_s[:].bitcast(I32), 0)
        load_scales(x_s, x_scales)
        w2_raw = placed(w2_room, 0, "w2_raw", [P, PACK, N], F32)
        load_weight(w2_raw, w2)
        x_w = sb("x_w", [P, TABLE], I32)
        load_words(x_w, x_words)
        w1_raw = sb("w1_raw", [P, PACK, N], F32)
        load_weight(w1_raw, w1)
        par_l = load_list("par_l", par)
        nxo_l = load_list("nxo_l", nxo)
        ident = sb("ident", [P, P], F32)
        make_identity(nc, ident[:])
        unit2_t = load_unit("unit2_t", unit2)
        unit_t = load_unit("unit_t", unit)

        rad_t = sb("rad_t", [P, TABLE], F32)
        for b in range(RAD_PER_PARTITION // TILES):
            spread = bank(b)
            for m in range(TILES):
                col = rad_cols[:, TILES * b + m : TILES * b + m + 1]
                nc.tensor.transpose(spread[:, block(m)], col.to_broadcast([P, P]), ident[:])
            nc.scalar.copy(
                rad_t[:].rearrange("p (n m) -> p n m", m=RAD_PER_PARTITION)[:, :, block(b, TILES)],
                spread[:].rearrange("p (m n) -> p n m", m=TILES),
            )
        unit_par = sb("unit_par", [P, PACK], F32)
        nc.gpsimd.tensor_scalar(unit_par[:], unit_t[:], 0.6, 0.0, ALU.mult, ALU.add)

        reach = sb("reach", [P, N], F32)

        def fetch_radius(name, tag, first, last):
            picked = sb(name, [P, last - first], F32, tag)
            nc.scalar.activation(picked[:], rad_t[:].indirect(entries(obs_l, first, last)), ACT.Copy)
            return picked

        def make_reach(picked, first, last):
            nc.scalar.activation(reach[:, first:last], picked[:], ACT.Exp, scale=2.0, bias=-0.2)

        make_reach(fetch_radius("rad_early", "rad_then_w3q", 0, EARLY), 0, EARLY)

        eq_s = sb("eq_s", [P, N], U8, "eq_s_then_rad")
        pick(eq_s, e_s[:], obs_l)
        w3_bf = sb("w3_bf", [P, PACK * N], BF16, "rounded")
        round_weight(w3_bf, w3_raw)
        eq_w = sb("eq_w", [P, N], U32, "w3_then_eq_w")
        pick(eq_w, e_w[:].bitcast(U32), obs_l)
        eq = (eq_w, eq_s)
        w3q = quantize("w3q", w3_bf, "rad_then_w3q")
        obst = sb("obst", [P, PACK, N], F32)
        for t in range(PACK):
            ye = bank(PACK + t)
            product(ye, w3q, block(t), eq)
            if t == PACK - 1:
                rad_late = fetch_radius("rad_late", "eq_s_then_rad", EARLY, N)
            nc.scalar.activation(obst[:, t, :], ye[:], ACT.Gelu_apprx_tanh)
        make_reach(rad_late, EARLY, N)

        w2_bf = sb("w2_bf", [P, PACK * N], BF16, "rounded")
        round_weight(w2_bf, w2_raw)
        xq_w = placed(w2_room, 0, "xq_w", [P, N], U32)
        xq_s = placed(w2_room, F32_TILE, "xq_s", [P, N], U8)
        pick(xq_s, x_s[:], offs_l)
        pick(xq_w, x_w[:].bitcast(U32), offs_l)
        xq = (xq_w, xq_s)

        hid2_planes = sb("hid2_planes", [P, PACK, N], F32)

        def scale_obst(engine, t):
            engine.tensor_scalar(hid2_planes[:, t, :], obst[:, t, :], unit2_t[:, t : t + 1], 0.0, ALU.mult, ALU.add)

        for t in range(PACK - 1):
            scale_obst(nc.gpsimd, t)
        w2q = quantize("w2q", w2_bf)
        yv = []
        for t in range(PACK):
            acc = bank(t)
            product(acc, w2q, block(t), xq)
            window = sb(f"yv{t}", [P, N], F32)
            nc.scalar.activation(window[:], acc[:], ACT.Copy, scale=unit_par[:, t : t + 1])
            yv.append(window)
        w1_bf = sb("w1_bf", [P, PACK * N], BF16, "rounded")
        round_weight(w1_bf, w1_raw)
        scale_obst(nc.vector, PACK - 1)
        w1q = quantize("w1q", w1_bf)
        y = []
        for t in range(PACK):
            acc = bank(PACK + t)
            product(acc, w1q, block(t), xq)
            y.append(acc)
        hid2 = weave(sb("hid2", [P, PACK * N], BF16, "hid2_then_planes"), hid2_planes[:])
        hid2q = quantize("hid2q", hid2)

        vp = [[sb(f"vp{h}_{t}", [P, HALF], F32) for t in range(PACK)] for h in range(2)]
        for h in range(2):
            for t in range(PACK):
                parents = yv[t][:].indirect(entries(par_l, h * HALF, (h + 1) * HALF))
                nc.scalar.activation(vp[h][t][:], parents, ACT.Copy)

        hid = [sb(f"hid{r}", [P, PACK * P], BF16, "hid_then_planes" if r == 0 else None) for r in range(TILES - 1)]
        hid.append(placed(expo_room, 2 * F32_TILE - PACK * P, f"hid{TILES - 1}", [P, PACK * P], BF16))
        hidq = []
        for h, tag in enumerate(("hid2_then_planes", "hid_then_planes")):
            planes = sb(f"hid_planes{h}", [P, PACK, HALF], F32, tag)
            for t in range(PACK):
                nc.vector.scalar_tensor_tensor(
                    planes[:, t, :], y[t][:, block(h, HALF)], unit_t[:, t : t + 1], vp[h][t][:], ALU.mult, ALU.add
                )
            woven = [weave(hid[2 * h + u], planes[:, :, block(u)]) for u in range(2)]
            hidq.extend([quantize(f"hidq{2 * h + u}", woven[u]) for u in range(2)])

        first_mag = sb("first_mag", [P, N], F32)
        later_mags = placed(pen_room, 3 * F32_TILE // 2, "later_mags", [P, TILES - 1, N], F32)
        decay = []
        for r in range(TILES):
            sc = bank(r)
            product(sc, hidq[r], block(0), hid2q)
            mag = first_mag[:] if r == 0 else later_mags[:, r - 1, :]
            nc.scalar.activation(mag, sc[:], ACT.Abs)
            decay.append(sb(f"decay{r}", [P, N], F32))
            nc.scalar.activation(decay[r][:], mag, ACT.Exp, scale=-2.0)

        def next_of(window, h):
            return window.indirect(entries(nxo_l, h * HALF, (h + 1) * HALF))

        expo = []
        for r in range(TILES):
            if r < PRE:
                both = placed(expo_room, r * 2 * F32_TILE, f"expo{r}", [P, 2 * N], F32)
                nc.vector.tensor_tensor(both[:, 0:N], decay[r][:], reach[:], ALU.mult)
                for h in range(2):
                    nc.vector.tensor_copy(both[:, block(2 + h, HALF)], next_of(both[:, 0:N], h))
                expo.append(both)
            else:
                expo.append(sb(f"expo{r}", [P, N], F32))
                nc.vector.tensor_tensor(expo[r][:], decay[r][:], reach[:], ALU.mult)

        pen = {}
        offset = 0
        for r in (0, 2, 3, 1):
            width = expo[r].shape[1]
            pen[r] = placed(pen_room, offset, f"pen{r}", [P, width], F32)
            nc.scalar.activation(pen[r][:], expo[r][:], ACT.Ln, bias=1.0)
            offset = offset + width * 4

        res = [sb(f"res{r}", [P, N], F32) for r in range(TILES)]

        def finish_gathered(r):
            nc.vector.scalar_tensor_tensor(res[r][:], pen[r][:, N : 2 * N], 0.5, pen[r][:, 0:N], ALU.mult, ALU.add)
            nc.sync.dma_start(out[block(r), :], res[r][:])

        finish_gathered(0)
        half_pen = sb("half_pen", [P, N], F32)
        nc.vector.tensor_scalar(half_pen[:], pen[2][:], 0.5, None, ALU.mult)
        for h in range(2):
            cols = block(h, HALF)
            nc.vector.tensor_tensor(res[2][:, cols], next_of(half_pen[:], h), pen[2][:, cols], ALU.add)
        nc.sync.dma_start(out[block(2), :], res[2][:])
        finish_gathered(1)
        nxt = sb("next3", [P, N], F32)
        for h in range(2):
            cols = block(h, HALF)
            nc.scalar.activation(nxt[:, cols], next_of(pen[3][:], h), ACT.Copy)
            nc.vector.scalar_tensor_tensor(res[3][:, cols], nxt[:, cols], 0.5, pen[3][:, cols], ALU.mult, ALU.add)
            nc.sync.dma_start(out[block(3), cols], res[3][:, cols])
